import numpy as np, ml_dtypes
CORES = [25,29,65,69,153,157,193,197]
N = 8
import mx_ref
NC, G = 256, 2
C = np.float32(0.043)
BF = ml_dtypes.bfloat16
def cut(t, i, w=512):
    return t[:, w * i:w * i + w]
def tile(rs):
    return np.stack(rs, axis=2).reshape(128, -1).astype(BF)
def layer(w, X):
    out = []
    for i in range(G):
        for t in range(len(X)):
            p = mx_ref.matmul(mx_ref.quantize(cut(w, len(X) * i + t)), X[t])
            z = p if t == 0 else z + p
        out.append(z)
    return out
def act(Z):
    return [np.maximum(s * z, 0) * C for z in Z for s in (1, -1)]
def setup_inputs(rng):
    def f(*shape):
        return mx_ref.flush((rng.standard_normal(shape, dtype=np.float32) * np.exp2(rng.integers(-2, 3, shape[:-1] + (1,)))).astype(BF))
    return {"x": f(N, 128, 4 * NC), "w1": f(N, 128, G * 512), "w2": f(N, 128, 512)}
def setup_inputs_blocks(rng):
    d = setup_inputs(rng)
    for k in ("x", "w1", "w2"): d[k] = mx_ref.spread(d[k], rng, 2)
    return d
def setup_inputs_wide(rng):
    d = setup_inputs(rng)
    for k in ("x", "w1", "w2"): d[k] = mx_ref.flush((d[k].astype(np.float32) * np.exp2(rng.integers(-6, 7, (N, 1, 1))).astype(np.float32)).astype(BF))
    return d
def reference(x, w1, w2):
    X = [mx_ref.quantize(x[j]) for j in range(N)]
    y = np.zeros((N, 128, NC), np.float32)
    for c in range(N):
        for r in range(N):
            p = mx_ref.matmul(mx_ref.quantize(w2[r]), mx_ref.quantize(tile(act(layer(w1[r], [X[c]])))))
            y[c] = p if r == 0 else y[c] + p
    return {"y": y}

@@ -1,0 +1,209 @@
+import numpy as np
+from concourse.bass import DstId, RemoteDMATransfer
+from concourse.mybir import dt, AluOpType, ActivationFunctionType
+
+N = 8
+WORLD = 256
+WC = 384
+NC = 256
+CS = float(np.float32(0.043))
+
+SCRATCH = {
+    "wbf": ("sbuf", [128, 4 * WC], "bfloat16"),
+    "xbf": ("sbuf", [128, 4 * NC], "bfloat16"),
+    "xq": ("sbuf", [128, NC], "float8_e4m3fn_x4"),
+    "xs": ("sbuf", [128, NC], "uint8"),
+    "wq": ("sbuf", [128, N * WC], "float8_e4m3fn_x4"),
+    "ws": ("sbuf", [128, N * WC], "uint8"),
+    "h0": ("sbuf", [128, 4 * NC], "bfloat16"),
+    "h1": ("sbuf", [128, 4 * NC], "bfloat16"),
+    "hq0": ("sbuf", [128, NC], "float8_e4m3fn_x4"),
+    "hq1": ("sbuf", [128, NC], "float8_e4m3fn_x4"),
+    "hs0": ("sbuf", [128, NC], "uint8"),
+    "hs1": ("sbuf", [128, NC], "uint8"),
+    "ysb": ("sbuf", [128, NC], "float32"),
+    "z": ("psum", [128, 512 * 4], "float32"),
+    "yacc": ("psum", [128, 512], "float32"),
+}
+SEMAPHORES = (["w", "x", "wq", "xq", "out", "done", "loc"]
+              + [n + b for n in ("za", "zb", "av", "as", "hq", "y") for b in "01"]
+              + ["p%d" % i for i in range(N)] + ["c%d" % i for i in range(N)])
+
+
+def _bits(mask):
+    return [e for e in range(mask.bit_length()) if (mask >> e) & 1]
+
+
+def _plan(cores, topo):
+    cores = list(cores)
+    own, fwd, relay = {}, {c: [] for c in cores}, {}
+    cls = {c: [] for c in cores}
+
+    def chipkey(c):
+        return (topo.host(c), topo.chip(c))
+
+    def groups(cs):
+        out = {}
+        for c in cs:
+            out.setdefault(chipkey(c), []).append(c)
+        return [out[k] for k in sorted(out)]
+
+    def common(src, dsts):
+        m = topo.mask(src, dsts[0])
+        for d in dsts[1:]:
+            m &= topo.mask(src, d)
+        return _bits(m)
+
+    for i, P in enumerate(cores):
+        lo, hi = i * WC, (i + 1) * WC
+        peers = [q for q in cores if q != P and chipkey(q) == chipkey(P)]
+        plane = [q for q in cores if topo.same_plane(P, q)]
+        cross = [q for q in cores if q != P and q not in peers and q not in plane]
+        off = common(P, plane)
+        on = [e for e in common(P, peers) if e not in off]
+        cls[P].append((0, i))
+        first, second = [], []
+        for grp in groups(cross):
+            near = topo.host(grp[0]) == topo.host(P)
+            if near:
+                rel = [k for k in range(WORLD) if chipkey(k) == chipkey(P) and k not in cores]
+            else:
+                rel = [k for k in range(WORLD) if topo.mates(k, grp[0]) and k not in cores and topo.may_write(P, k)]
+            rel = [k for k in rel if topo.die(k) == topo.die(P) and all(topo.may_write(k, d) for d in grp)][:2]
+            pool = on if near else off
+            ne, nc = len(pool) // len(rel), WC // len(rel)
+            for t, k in enumerate(rel):
+                a, b = lo + t * nc, lo + (t + 1) * nc
+                first.append(([k], pool[t * ne:(t + 1) * ne], a, b, i))
+                out = [(grp, common(k, grp), a, b, i)]
+                relay[k] = [(i, "p", out), (i, "c", out)]
+            for d in grp:
+                cls[d].append((3 if near else 4, i))
+        second.append((peers, on, lo, hi, i))
+        for d in peers:
+            cls[d].append((1, i))
+        for grp in groups(plane):
+            head = [d for d in grp if topo.die(d) == topo.die(P)][0]
+            rest = [d for d in grp if d != head]
+            second.append(([head], off, lo, hi, i))
+            cls[head].append((2, i))
+            out = [(rest, common(head, rest), lo, hi, i)]
+            fwd[head] += [(i, "p", out), (i, "c", out)]
+            for d in rest:
+                cls[d].append((5, i))
+        own[P] = [(None, "p", first), (None, "c", first), (None, "p", second), (None, "c", second)]
+
+    steps = dict(relay)
+    for P in cores:
+        steps[P] = own[P] + fwd[P]
+    expect = {}
+    for c in steps:
+        for _, kind, trs in steps[c]:
+            for dsts, engs, _, _, slot in trs:
+                expect[(c, "loc")] = expect.get((c, "loc"), 0) + len(engs)
+                for d in dsts:
+                    key = (d, "%s%d" % (kind, slot))
+                    expect[key] = expect.get(key, 0) + len(engs)
+    order = {c: [s for _, s in sorted(cls[c])] for c in cores}
+    return steps, expect, order
+
+
+def _remote(g, core, T, topo, steps, expect):
+    for wait, kind, trs in steps:
+        if wait is not None:
+            name = "%s%d" % (kind, wait)
+            g.wait_ge(T.sem[name], expect[(core, name)])
+        calls = []
+        for dsts, engs, a, b, slot in trs:
+            def view():
+                return T.ws[:, a:b] if kind == "p" else T.wq[:, a:b].bitcast(dt.uint8)
+            ids = []
+            for d in dsts:
+                rid, pid = topo.addr(d, core)
+                ids.append(DstId(rid=rid, pnc=pid))
+            calls.append(RemoteDMATransfer(dst_ids=ids, dma_engine_mask=sum(1 << e for e in engs),
+                                           remote_sem=T.sem["%s%d" % (kind, slot)],
+                                           srcs=[view()], dsts=[view() for _ in dsts]))
+        g.remote_dma_fused(calls, local_sem=T.sem.loc)
+    g.wait_ge(T.sem.loc, expect[(core, "loc")])
+
+
+def _compute(g, core, T, slots, expect):
+    sem, te, ve, sc = T.sem, g.tensor, g.vector, g.scalar
+    o = slots[0] * WC
+    g.sync.dma_start(T.wbf[:, 0:1024], T.w1[:]).then_inc(sem.w, 16)
+    g.scalar.dma_start(T.wbf[:, 1024:1536], T.w2[:]).then_inc(sem.w, 16)
+    g.sync.dma_start(T.xbf[:], T.x[:]).then_inc(sem.x, 16)
+    ve.wait_ge(sem.w, 32)
+    ve.quantize_mx(T.wq[:, o:o + WC], T.ws[:, o:o + WC], T.wbf[:]).then_inc(sem.wq, 1)
+    ve.wait_ge(sem.x, 16)
+    ve.quantize_mx(T.xq[:], T.xs[:], T.xbf[:]).then_inc(sem.xq, 1)
+
+    def s(name, k):
+        return sem["%s%d" % (name, k % 2)]
+
+    def bank(k, i):
+        c = 512 * (2 * (k % 2) + i)
+        return T.z[:, c:c + NC]
+
+    def first_layer(k):
+        w, m = slots[k] * WC, k // 2
+        if k == 0:
+            te.wait_ge(sem.wq, 1)
+            te.wait_ge(sem.xq, 1)
+        else:
+            for kind in "pc":
+                name = "%s%d" % (kind, slots[k])
+                te.wait_ge(sem[name], expect[(core, name)])
+        for i, (free, made) in enumerate((("av", "za"), ("as", "zb"))):
+            if m:
+                te.wait_ge(s(free, k), 2 * m)
+            a = w + 128 * i
+            te.matmul_mx(bank(k, i), T.wq[:, a:a + 128], T.ws[:, a:a + 128], T.xq[:], T.xs[:], True, True
+                         ).then_inc(s(made, k), 1)
+
+    def tile(k):
+        m, h = k // 2, T["h%d" % (k % 2)]
+        ve.wait_ge(s("za", k), m + 1)
+        sc.wait_ge(s("zb", k), m + 1)
+        if m:
+            ve.wait_ge(s("hq", k), m)
+            sc.wait_ge(s("hq", k), m)
+        ve.tensor_scalar(h[:, 0:4 * NC:4], bank(k, 0), 0.0, CS, AluOpType.max, AluOpType.mult).then_inc(s("av", k), 1)
+        ve.tensor_scalar(h[:, 1:4 * NC:4], bank(k, 0), -CS, 0.0, AluOpType.mult, AluOpType.max).then_inc(s("av", k), 1)
+        sc.activation(h[:, 2:4 * NC:4], bank(k, 1), ActivationFunctionType.Relu, scale=CS).then_inc(s("as", k), 1)
+        sc.activation(h[:, 3:4 * NC:4], bank(k, 1), ActivationFunctionType.Relu, scale=-CS).then_inc(s("as", k), 1)
+        ve.wait_ge(s("av", k), 2 * (m + 1))
+        ve.wait_ge(s("as", k), 2 * (m + 1))
+        if m:
+            ve.wait_ge(s("y", k), m)
+        ve.quantize_mx(T["hq%d" % (k % 2)][:], T["hs%d" % (k % 2)][:], h[:]).then_inc(s("hq", k), 1)
+
+    def second_layer(k):
+        a = slots[k] * WC + 256
+        te.wait_ge(s("hq", k), k // 2 + 1)
+        te.matmul_mx(T.yacc[:, 0:NC], T.wq[:, a:a + 128], T.ws[:, a:a + 128],
+                     T["hq%d" % (k % 2)][:], T["hs%d" % (k % 2)][:], k == 0, k == N - 1).then_inc(s("y", k), 1)
+
+    for k in range(N):
+        first_layer(k)
+        if k:
+            second_layer(k - 1)
+        tile(k)
+    second_layer(N - 1)
+    ve.wait_ge(sem.y0, N // 2)
+    ve.wait_ge(sem.y1, N // 2)
+    ve.tensor_copy(T.ysb[:], T.yacc[:, 0:NC]).then_inc(sem.out, 1)
+    g.sync.wait_ge(sem.out, 1)
+    g.sync.dma_start(T.y[:], T.ysb[:]).then_inc(sem.done, 16)
+    g.sync.wait_ge(sem.done, 16)
+
+
+def rank_program(g, core, T, topo):
+    steps, expect, order = _plan(T.cores, topo)
+    if core not in steps:
+        return
+    if T.rank_of(core) is not None:
+        _compute(g, core, T, order[core], expect)
+        g.wait_ge(T.sem.wq, 1)
+    _remote(g, core, T, topo, steps[core], expect)

@@ -5,8 +5,11 @@ from concourse.mybir import dt, AluOpType, ActivationFunctionType
 N = 8
 WORLD = 256
 WC = 384
+W1C = 256
 NC = 256
 CS = float(np.float32(0.043))
+SETS = 3
+AHEAD = 2
 
 SCRATCH = {
     "wbf": ("sbuf", [128, 4 * WC], "bfloat16"),
@@ -15,19 +18,17 @@ SCRATCH = {
     "xs": ("sbuf", [128, NC], "uint8"),
     "wq": ("sbuf", [128, N * WC], "float8_e4m3fn_x4"),
     "ws": ("sbuf", [128, N * WC], "uint8"),
-    "h0": ("sbuf", [128, 4 * NC], "bfloat16"),
-    "h1": ("sbuf", [128, 4 * NC], "bfloat16"),
-    "hq0": ("sbuf", [128, NC], "float8_e4m3fn_x4"),
-    "hq1": ("sbuf", [128, NC], "float8_e4m3fn_x4"),
-    "hs0": ("sbuf", [128, NC], "uint8"),
-    "hs1": ("sbuf", [128, NC], "uint8"),
     "ysb": ("sbuf", [128, NC], "float32"),
-    "z": ("psum", [128, 512 * 4], "float32"),
+    "z": ("psum", [128, 512 * 2 * SETS], "float32"),
     "yacc": ("psum", [128, 512], "float32"),
 }
-SEMAPHORES = (["w", "x", "wq", "xq", "out", "done", "loc"]
-              + [n + b for n in ("za", "zb", "av", "as", "hq", "y") for b in "01"]
-              + ["p%d" % i for i in range(N)] + ["c%d" % i for i in range(N)])
+for _b in range(SETS):
+    SCRATCH["h%d" % _b] = ("sbuf", [128, 4 * NC], "bfloat16")
+    SCRATCH["hq%d" % _b] = ("sbuf", [128, NC], "float8_e4m3fn_x4")
+    SCRATCH["hs%d" % _b] = ("sbuf", [128, NC], "uint8")
+SEMAPHORES = (["w1", "w2", "x", "wqa", "wqb", "xq", "out", "done", "loc"]
+              + ["%s%d" % (n, b) for n in ("za", "zb", "av", "as", "hq", "y") for b in range(SETS)]
+              + ["a%d" % i for i in range(N)] + ["b%d" % i for i in range(N)])
 
 
 def _bits(mask):
@@ -56,13 +57,28 @@ def _plan(cores, topo):
 
     for i, P in enumerate(cores):
         lo, hi = i * WC, (i + 1) * WC
+        sa, sb = "a%d" % i, "b%d" % i
+        parts = ((lo, lo + W1C, sa), (lo + W1C, hi, sb))
         peers = [q for q in cores if q != P and chipkey(q) == chipkey(P)]
         plane = [q for q in cores if topo.same_plane(P, q)]
         cross = [q for q in cores if q != P and q not in peers and q not in plane]
         off = common(P, plane)
         on = [e for e in common(P, peers) if e not in off]
         cls[P].append((0, i))
-        first, second = [], []
+        direct = [(peers, on)]
+        for d in peers:
+            cls[d].append((1, i))
+        for grp in groups(plane):
+            head = [d for d in grp if topo.die(d) == topo.die(P)][0]
+            rest = [d for d in grp if d != head]
+            direct.append(([head], off))
+            cls[head].append((2, i))
+            for a, b, sn in parts:
+                out = [(rest, common(head, rest), a, b, sn)]
+                fwd[head] += [(sn, "p", out), (None, "c", out)]
+            for d in rest:
+                cls[d].append((3, i))
+        far = []
         for grp in groups(cross):
             near = topo.host(grp[0]) == topo.host(P)
             if near:
@@ -74,36 +90,29 @@ def _plan(cores, topo):
             ne, nc = len(pool) // len(rel), WC // len(rel)
             for t, k in enumerate(rel):
                 a, b = lo + t * nc, lo + (t + 1) * nc
-                first.append(([k], pool[t * ne:(t + 1) * ne], a, b, i))
-                out = [(grp, common(k, grp), a, b, i)]
-                relay[k] = [(i, "p", out), (i, "c", out)]
+                far.append((k, pool[t * ne:(t + 1) * ne], a, b))
+                out = [(grp, common(k, grp), a, b, sa)]
+                relay[k] = [(sa, "p", out), (sb, "c", out)]
             for d in grp:
-                cls[d].append((3 if near else 4, i))
-        second.append((peers, on, lo, hi, i))
-        for d in peers:
-            cls[d].append((1, i))
-        for grp in groups(plane):
-            head = [d for d in grp if topo.die(d) == topo.die(P)][0]
-            rest = [d for d in grp if d != head]
-            second.append(([head], off, lo, hi, i))
-            cls[head].append((2, i))
-            out = [(rest, common(head, rest), lo, hi, i)]
-            fwd[head] += [(i, "p", out), (i, "c", out)]
-            for d in rest:
-                cls[d].append((5, i))
-        own[P] = [(None, "p", first), (None, "c", first), (None, "p", second), (None, "c", second)]
+                cls[d].append((4 if near else 5, i))
+        own[P] = []
+        for (a, b, sn), ready in zip(parts, ("wqa", "wqb")):
+            trs = [(dsts, engs, a, b, sn) for dsts, engs in direct]
+            own[P] += [(ready, "p", trs), (None, "c", trs)]
+        own[P] += [(None, "p", [([k], e, a, b, sa) for k, e, a, b in far]),
+                   (None, "c", [([k], e, a, b, sb) for k, e, a, b in far])]
 
     steps = dict(relay)
+    expect = {}
     for P in cores:
         steps[P] = own[P] + fwd[P]
-    expect = {}
+        expect[(P, "wqa")] = expect[(P, "wqb")] = 1
     for c in steps:
         for _, kind, trs in steps[c]:
-            for dsts, engs, _, _, slot in trs:
+            for dsts, engs, _, _, sn in trs:
                 expect[(c, "loc")] = expect.get((c, "loc"), 0) + len(engs)
                 for d in dsts:
-                    key = (d, "%s%d" % (kind, slot))
-                    expect[key] = expect.get(key, 0) + len(engs)
+                    expect[(d, sn)] = expect.get((d, sn), 0) + len(engs)
     order = {c: [s for _, s in sorted(cls[c])] for c in cores}
     return steps, expect, order
 
@@ -111,10 +120,9 @@ def _plan(cores, topo):
 def _remote(g, core, T, topo, steps, expect):
     for wait, kind, trs in steps:
         if wait is not None:
-            name = "%s%d" % (kind, wait)
-            g.wait_ge(T.sem[name], expect[(core, name)])
+            g.wait_ge(T.sem[wait], expect[(core, wait)])
         calls = []
-        for dsts, engs, a, b, slot in trs:
+        for dsts, engs, a, b, sn in trs:
             def view():
                 return T.ws[:, a:b] if kind == "p" else T.wq[:, a:b].bitcast(dt.uint8)
             ids = []
@@ -122,8 +130,7 @@ def _remote(g, core, T, topo, steps, expect):
                 rid, pid = topo.addr(d, core)
                 ids.append(DstId(rid=rid, pnc=pid))
             calls.append(RemoteDMATransfer(dst_ids=ids, dma_engine_mask=sum(1 << e for e in engs),
-                                           remote_sem=T.sem["%s%d" % (kind, slot)],
-                                           srcs=[view()], dsts=[view() for _ in dsts]))
+                                           remote_sem=T.sem[sn], srcs=[view()], dsts=[view() for _ in dsts]))
         g.remote_dma_fused(calls, local_sem=T.sem.loc)
     g.wait_ge(T.sem.loc, expect[(core, "loc")])
 
@@ -131,30 +138,33 @@ def _remote(g, core, T, topo, steps, expect):
 def _compute(g, core, T, slots, expect):
     sem, te, ve, sc = T.sem, g.tensor, g.vector, g.scalar
     o = slots[0] * WC
-    g.sync.dma_start(T.wbf[:, 0:1024], T.w1[:]).then_inc(sem.w, 16)
-    g.scalar.dma_start(T.wbf[:, 1024:1536], T.w2[:]).then_inc(sem.w, 16)
+    g.sync.dma_start(T.wbf[:, 0:4 * W1C], T.w1[:]).then_inc(sem.w1, 16)
+    g.scalar.dma_start(T.wbf[:, 4 * W1C:4 * WC], T.w2[:]).then_inc(sem.w2, 16)
     g.sync.dma_start(T.xbf[:], T.x[:]).then_inc(sem.x, 16)
-    ve.wait_ge(sem.w, 32)
-    ve.quantize_mx(T.wq[:, o:o + WC], T.ws[:, o:o + WC], T.wbf[:]).then_inc(sem.wq, 1)
+    ve.wait_ge(sem.w1, 16)
+    ve.quantize_mx(T.wq[:, o:o + W1C], T.ws[:, o:o + W1C], T.wbf[:, 0:4 * W1C]).then_inc(sem.wqa, 1)
+    ve.wait_ge(sem.w2, 16)
+    ve.quantize_mx(T.wq[:, o + W1C:o + WC], T.ws[:, o + W1C:o + WC], T.wbf[:, 4 * W1C:4 * WC]).then_inc(sem.wqb, 1)
     ve.wait_ge(sem.x, 16)
     ve.quantize_mx(T.xq[:], T.xs[:], T.xbf[:]).then_inc(sem.xq, 1)
 
     def s(name, k):
-        return sem["%s%d" % (name, k % 2)]
+        return sem["%s%d" % (name, k % SETS)]
 
     def bank(k, i):
-        c = 512 * (2 * (k % 2) + i)
+        c = 512 * (2 * (k % SETS) + i)
         return T.z[:, c:c + NC]
 
+    def arrived(k, part):
+        name = ("wq%s" % part) if k == 0 else "%s%d" % (part, slots[k])
+        if (core, name) in expect:
+            te.wait_ge(sem[name], expect[(core, name)])
+
     def first_layer(k):
-        w, m = slots[k] * WC, k // 2
+        w, m = slots[k] * WC, k // SETS
+        arrived(k, "a")
         if k == 0:
-            te.wait_ge(sem.wq, 1)
             te.wait_ge(sem.xq, 1)
-        else:
-            for kind in "pc":
-                name = "%s%d" % (kind, slots[k])
-                te.wait_ge(sem[name], expect[(core, name)])
         for i, (free, made) in enumerate((("av", "za"), ("as", "zb"))):
             if m:
                 te.wait_ge(s(free, k), 2 * m)
@@ -163,7 +173,7 @@ def _compute(g, core, T, slots, expect):
                          ).then_inc(s(made, k), 1)
 
     def tile(k):
-        m, h = k // 2, T["h%d" % (k % 2)]
+        m, h = k // SETS, T["h%d" % (k % SETS)]
         ve.wait_ge(s("za", k), m + 1)
         sc.wait_ge(s("zb", k), m + 1)
         if m:
@@ -177,22 +187,24 @@ def _compute(g, core, T, slots, expect):
         ve.wait_ge(s("as", k), 2 * (m + 1))
         if m:
             ve.wait_ge(s("y", k), m)
-        ve.quantize_mx(T["hq%d" % (k % 2)][:], T["hs%d" % (k % 2)][:], h[:]).then_inc(s("hq", k), 1)
+        ve.quantize_mx(T["hq%d" % (k % SETS)][:], T["hs%d" % (k % SETS)][:], h[:]).then_inc(s("hq", k), 1)
 
     def second_layer(k):
-        a = slots[k] * WC + 256
-        te.wait_ge(s("hq", k), k // 2 + 1)
+        a = slots[k] * WC + W1C
+        arrived(k, "b")
+        te.wait_ge(s("hq", k), k // SETS + 1)
         te.matmul_mx(T.yacc[:, 0:NC], T.wq[:, a:a + 128], T.ws[:, a:a + 128],
-                     T["hq%d" % (k % 2)][:], T["hs%d" % (k % 2)][:], k == 0, k == N - 1).then_inc(s("y", k), 1)
+                     T["hq%d" % (k % SETS)][:], T["hs%d" % (k % SETS)][:], k == 0, k == N - 1).then_inc(s("y", k), 1)
 
     for k in range(N):
         first_layer(k)
-        if k:
-            second_layer(k - 1)
+        if k >= AHEAD:
+            second_layer(k - AHEAD)
         tile(k)
-    second_layer(N - 1)
-    ve.wait_ge(sem.y0, N // 2)
-    ve.wait_ge(sem.y1, N // 2)
+    for k in range(N - AHEAD, N):
+        second_layer(k)
+    for b in range(SETS):
+        ve.wait_ge(sem["y%d" % b], len(range(b, N, SETS)))
     ve.tensor_copy(T.ysb[:], T.yacc[:, 0:NC]).then_inc(sem.out, 1)
     g.sync.wait_ge(sem.out, 1)
     g.sync.dma_start(T.y[:], T.ysb[:]).then_inc(sem.done, 16)
@@ -205,5 +217,4 @@ def rank_program(g, core, T, topo):
         return
     if T.rank_of(core) is not None:
         _compute(g, core, T, order[core], expect)
-        g.wait_ge(T.sem.wq, 1)
     _remote(g, core, T, topo, steps[core], expect)

@@ -68,33 +68,44 @@ def _plan(cores, topo):
         direct = [(peers, on)]
         for d in peers:
             cls[d].append((1, i))
-        for grp in groups(plane):
+
+        def split(grp):
             head = [d for d in grp if topo.die(d) == topo.die(P)][0]
-            rest = [d for d in grp if d != head]
+            return head, [d for d in grp if d != head]
+
+        for grp in groups(plane):
+            head, rest = split(grp)
             direct.append(([head], off))
             cls[head].append((2, i))
+            sts = []
             for a, b, sn in parts:
                 out = [(rest, common(head, rest), a, b, sn)]
-                fwd[head] += [(sn, "p", out), (None, "c", out)]
+                sts += [(sn, "p", out), (None, "c", out)]
+            fwd[head].append((2, sts))
             for d in rest:
                 cls[d].append((3, i))
         far = []
         for grp in groups(cross):
             near = topo.host(grp[0]) == topo.host(P)
+            head, rest = split(grp)
             if near:
                 rel = [k for k in range(WORLD) if chipkey(k) == chipkey(P) and k not in cores]
             else:
-                rel = [k for k in range(WORLD) if topo.mates(k, grp[0]) and k not in cores and topo.may_write(P, k)]
-            rel = [k for k in rel if topo.die(k) == topo.die(P) and all(topo.may_write(k, d) for d in grp)][:2]
+                rel = [k for k in range(WORLD) if topo.mates(k, head) and k not in cores and topo.may_write(P, k)]
+            rel = [k for k in rel if topo.die(k) == topo.die(P) and topo.may_write(k, head)][:2]
             pool = on if near else off
             ne, nc = len(pool) // len(rel), WC // len(rel)
             for t, k in enumerate(rel):
                 a, b = lo + t * nc, lo + (t + 1) * nc
                 far.append((k, pool[t * ne:(t + 1) * ne], a, b))
-                out = [(grp, common(k, grp), a, b, sa)]
-                relay[k] = [(sa, "p", out), (sb, "c", out)]
-            for d in grp:
-                cls[d].append((4 if near else 5, i))
+                e = common(k, [head])
+                relay[k] = [(sa, "p", [([head], e, a, b, sa)]), (sb, "c", [([head], e, a, b, sb)])]
+            e = common(head, rest)
+            fwd[head].append((4 if near else 5,
+                              [(sa, "p", [(rest, e, lo, hi, sa)]), (sb, "c", [(rest, e, lo, hi, sb)])]))
+            cls[head].append((4 if near else 5, i))
+            for d in rest:
+                cls[d].append((6 if near else 7, i))
         own[P] = []
         for (a, b, sn), ready in zip(parts, ("wqa", "wqb")):
             trs = [(dsts, engs, a, b, sn) for dsts, engs in direct]
@@ -105,7 +116,7 @@ def _plan(cores, topo):
     steps = dict(relay)
     expect = {}
     for P in cores:
-        steps[P] = own[P] + fwd[P]
+        steps[P] = own[P] + [st for _, sts in sorted(fwd[P], key=lambda f: f[0]) for st in sts]
         expect[(P, "wqa")] = expect[(P, "wqb")] = 1
     for c in steps:
         for _, kind, trs in steps[c]:
@@ -113,7 +124,7 @@ def _plan(cores, topo):
                 expect[(c, "loc")] = expect.get((c, "loc"), 0) + len(engs)
                 for d in dsts:
                     expect[(d, sn)] = expect.get((d, sn), 0) + len(engs)
-    order = {c: [s for _, s in sorted(cls[c])] for c in cores}
+    order = {c: sorted(cls[c]) for c in cores}
     return steps, expect, order
 
 
@@ -135,8 +146,9 @@ def _remote(g, core, T, topo, steps, expect):
     g.wait_ge(T.sem.loc, expect[(core, "loc")])
 
 
-def _compute(g, core, T, slots, expect):
+def _compute(g, core, T, order, expect):
     sem, te, ve, sc = T.sem, g.tensor, g.vector, g.scalar
+    slots = [sl for _, sl in order]
     o = slots[0] * WC
     g.sync.dma_start(T.wbf[:, 0:4 * W1C], T.w1[:]).then_inc(sem.w1, 16)
     g.scalar.dma_start(T.wbf[:, 4 * W1C:4 * WC], T.w2[:]).then_inc(sem.w2, 16)
@@ -157,12 +169,13 @@ def _compute(g, core, T, slots, expect):
 
     def arrived(k, part):
         name = ("wq%s" % part) if k == 0 else "%s%d" % (part, slots[k])
-        if (core, name) in expect:
-            te.wait_ge(sem[name], expect[(core, name)])
+        te.wait_ge(sem[name], expect[(core, name)])
 
     def first_layer(k):
         w, m = slots[k] * WC, k // SETS
         arrived(k, "a")
+        if order[k][0] >= 4:
+            arrived(k, "b")
         if k == 0:
             te.wait_ge(sem.xq, 1)
         for i, (free, made) in enumerate((("av", "za"), ("as", "zb"))):
@@ -191,7 +204,8 @@ def _compute(g, core, T, slots, expect):
 
     def second_layer(k):
         a = slots[k] * WC + W1C
-        arrived(k, "b")
+        if order[k][0] < 4:
+            arrived(k, "b")
         te.wait_ge(s("hq", k), k // SETS + 1)
         te.matmul_mx(T.yacc[:, 0:NC], T.wq[:, a:a + 128], T.ws[:, a:a + 128],
                      T["hq%d" % (k % SETS)][:], T["hs%d" % (k % SETS)][:], k == 0, k == N - 1).then_inc(s("y", k), 1)

@@ -9,7 +9,7 @@ W1C = 256
 NC = 256
 CS = float(np.float32(0.043))
 SETS = 3
-AHEAD = 2
+LAG = 3
 
 SCRATCH = {
     "wbf": ("sbuf", [128, 4 * WC], "bfloat16"),
@@ -22,13 +22,13 @@ SCRATCH = {
     "z": ("psum", [128, 512 * 2 * SETS], "float32"),
     "yacc": ("psum", [128, 512], "float32"),
 }
-for _b in range(SETS):
+for _b in range(N):
     SCRATCH["h%d" % _b] = ("sbuf", [128, 4 * NC], "bfloat16")
     SCRATCH["hq%d" % _b] = ("sbuf", [128, NC], "float8_e4m3fn_x4")
     SCRATCH["hs%d" % _b] = ("sbuf", [128, NC], "uint8")
-SEMAPHORES = (["w1", "w2", "x", "wqa", "wqb", "xq", "out", "done", "loc"]
-              + ["%s%d" % (n, b) for n in ("za", "zb", "av", "as", "hq", "y") for b in range(SETS)]
-              + ["a%d" % i for i in range(N)] + ["b%d" % i for i in range(N)])
+SEMAPHORES = (["w1a", "w1b", "w2", "x", "wq0", "wq1", "wqb", "xq", "y", "out", "done", "loc"]
+              + ["%s%d" % (n, b) for n in ("za", "zb", "av", "as", "hq") for b in range(N)]
+              + ["%s%d" % (n, i) for n in ("a", "b", "c") for i in range(N)])
 
 
 def _bits(mask):
@@ -57,8 +57,8 @@ def _plan(cores, topo):
 
     for i, P in enumerate(cores):
         lo, hi = i * WC, (i + 1) * WC
-        sa, sb = "a%d" % i, "b%d" % i
-        parts = ((lo, lo + W1C, sa), (lo + W1C, hi, sb))
+        sa, sb, sc = "a%d" % i, "b%d" % i, "c%d" % i
+        mid = lo + W1C // 2
         peers = [q for q in cores if q != P and chipkey(q) == chipkey(P)]
         plane = [q for q in cores if topo.same_plane(P, q)]
         cross = [q for q in cores if q != P and q not in peers and q not in plane]
@@ -77,14 +77,12 @@ def _plan(cores, topo):
             head, rest = split(grp)
             direct.append(([head], off))
             cls[head].append((2, i))
-            sts = []
-            for a, b, sn in parts:
+            for a, b, sn, need, when in ((lo, lo + W1C, sa, (sa, sc), 2), (lo + W1C, hi, sb, (sb,), 5)):
                 out = [(rest, common(head, rest), a, b, sn)]
-                sts += [(sn, "p", out), (None, "c", out)]
-            fwd[head].append((2, sts))
+                fwd[head].append((when, [(need, "p", out), ((), "c", out)]))
             for d in rest:
                 cls[d].append((3, i))
-        far = []
+        feed = []
         for grp in groups(cross):
             near = topo.host(grp[0]) == topo.host(P)
             head, rest = split(grp)
@@ -97,27 +95,32 @@ def _plan(cores, topo):
             ne, nc = len(pool) // len(rel), WC // len(rel)
             for t, k in enumerate(rel):
                 a, b = lo + t * nc, lo + (t + 1) * nc
-                far.append((k, pool[t * ne:(t + 1) * ne], a, b))
+                feed.append((k, pool[t * ne:(t + 1) * ne], a, b))
                 e = common(k, [head])
-                relay[k] = [(sa, "p", [([head], e, a, b, sa)]), (sb, "c", [([head], e, a, b, sb)])]
+                relay[k] = [((sa,), "p", [([head], e, a, b, sa)]), ((sb,), "c", [([head], e, a, b, sb)])]
             e = common(head, rest)
-            fwd[head].append((4 if near else 5,
-                              [(sa, "p", [(rest, e, lo, hi, sa)]), (sb, "c", [(rest, e, lo, hi, sb)])]))
+            fwd[head].append((4 if near else 6,
+                              [((sa,), "p", [(rest, e, lo, hi, sa)]), ((sb,), "c", [(rest, e, lo, hi, sb)])]))
             cls[head].append((4 if near else 5, i))
             for d in rest:
                 cls[d].append((6 if near else 7, i))
-        own[P] = []
-        for (a, b, sn), ready in zip(parts, ("wqa", "wqb")):
-            trs = [(dsts, engs, a, b, sn) for dsts, engs in direct]
-            own[P] += [(ready, "p", trs), (None, "c", trs)]
-        own[P] += [(None, "p", [([k], e, a, b, sa) for k, e, a, b in far]),
-                   (None, "c", [([k], e, a, b, sb) for k, e, a, b in far])]
+
+        def straight(need, kind, a, b, sn):
+            return (need, kind, [(dsts, engs, a, b, sn) for dsts, engs in direct])
+
+        own[P] = [straight(("wq0",), "c", lo, mid, sa),
+                  straight(("wq1",), "p", lo, lo + W1C, sa),
+                  straight((), "c", mid, lo + W1C, sc),
+                  (("wqb",), "p", [([k], e, a, b, sa) for k, e, a, b in feed]),
+                  ((), "c", [([k], e, a, b, sb) for k, e, a, b in feed]),
+                  straight((), "p", lo + W1C, hi, sb),
+                  straight((), "c", lo + W1C, hi, sb)]
 
     steps = dict(relay)
     expect = {}
     for P in cores:
         steps[P] = own[P] + [st for _, sts in sorted(fwd[P], key=lambda f: f[0]) for st in sts]
-        expect[(P, "wqa")] = expect[(P, "wqb")] = 1
+        expect[(P, "wq0")] = expect[(P, "wq1")] = expect[(P, "wqb")] = 1
     for c in steps:
         for _, kind, trs in steps[c]:
             for dsts, engs, _, _, sn in trs:
@@ -129,8 +132,8 @@ def _plan(cores, topo):
 
 
 def _remote(g, core, T, topo, steps, expect):
-    for wait, kind, trs in steps:
-        if wait is not None:
+    for waits, kind, trs in steps:
+        for wait in waits:
             g.wait_ge(T.sem[wait], expect[(core, wait)])
         calls = []
         for dsts, engs, a, b, sn in trs:
@@ -150,75 +153,85 @@ def _compute(g, core, T, order, expect):
     sem, te, ve, sc = T.sem, g.tensor, g.vector, g.scalar
     slots = [sl for _, sl in order]
     o = slots[0] * WC
-    g.sync.dma_start(T.wbf[:, 0:4 * W1C], T.w1[:]).then_inc(sem.w1, 16)
-    g.scalar.dma_start(T.wbf[:, 4 * W1C:4 * WC], T.w2[:]).then_inc(sem.w2, 16)
+    H = W1C // 2
+    g.sync.dma_start(T.wbf[:, 0:4 * H], T.w1[:, 0:4 * H]).then_inc(sem.w1a, 16)
+    g.sync.dma_start(T.wbf[:, 4 * H:4 * W1C], T.w1[:, 4 * H:4 * W1C]).then_inc(sem.w1b, 16)
+    g.sync.dma_start(T.wbf[:, 4 * W1C:4 * WC], T.w2[:]).then_inc(sem.w2, 16)
     g.sync.dma_start(T.xbf[:], T.x[:]).then_inc(sem.x, 16)
-    ve.wait_ge(sem.w1, 16)
-    ve.quantize_mx(T.wq[:, o:o + W1C], T.ws[:, o:o + W1C], T.wbf[:, 0:4 * W1C]).then_inc(sem.wqa, 1)
+    ve.wait_ge(sem.w1a, 16)
+    ve.quantize_mx(T.wq[:, o:o + H], T.ws[:, o:o + H], T.wbf[:, 0:4 * H]).then_inc(sem.wq0, 1)
+    ve.wait_ge(sem.w1b, 16)
+    ve.quantize_mx(T.wq[:, o + H:o + W1C], T.ws[:, o + H:o + W1C], T.wbf[:, 4 * H:4 * W1C]).then_inc(sem.wq1, 1)
     ve.wait_ge(sem.w2, 16)
     ve.quantize_mx(T.wq[:, o + W1C:o + WC], T.ws[:, o + W1C:o + WC], T.wbf[:, 4 * W1C:4 * WC]).then_inc(sem.wqb, 1)
     ve.wait_ge(sem.x, 16)
     ve.quantize_mx(T.xq[:], T.xs[:], T.xbf[:]).then_inc(sem.xq, 1)
 
     def s(name, k):
-        return sem["%s%d" % (name, k % SETS)]
+        return sem["%s%d" % (name, k)]
 
     def bank(k, i):
         c = 512 * (2 * (k % SETS) + i)
         return T.z[:, c:c + NC]
 
     def arrived(k, part):
-        name = ("wq%s" % part) if k == 0 else "%s%d" % (part, slots[k])
+        name = {"a": "wq0", "c": "wq1", "b": "wqb"}[part] if k == 0 else "%s%d" % (part, slots[k])
         te.wait_ge(sem[name], expect[(core, name)])
 
     def first_layer(k):
-        w, m = slots[k] * WC, k // SETS
+        w = slots[k] * WC
         arrived(k, "a")
         if order[k][0] >= 4:
             arrived(k, "b")
         if k == 0:
             te.wait_ge(sem.xq, 1)
         for i, (free, made) in enumerate((("av", "za"), ("as", "zb"))):
-            if m:
-                te.wait_ge(s(free, k), 2 * m)
+            if i == 1 and order[k][0] <= 2:
+                arrived(k, "c")
+            if k >= SETS:
+                te.wait_ge(s(free, k - SETS), 2)
             a = w + 128 * i
             te.matmul_mx(bank(k, i), T.wq[:, a:a + 128], T.ws[:, a:a + 128], T.xq[:], T.xs[:], True, True
                          ).then_inc(s(made, k), 1)
 
     def tile(k):
-        m, h = k // SETS, T["h%d" % (k % SETS)]
-        ve.wait_ge(s("za", k), m + 1)
-        sc.wait_ge(s("zb", k), m + 1)
-        if m:
-            ve.wait_ge(s("hq", k), m)
-            sc.wait_ge(s("hq", k), m)
+        h = T["h%d" % k]
+        ve.wait_ge(s("za", k), 1)
         ve.tensor_scalar(h[:, 0:4 * NC:4], bank(k, 0), 0.0, CS, AluOpType.max, AluOpType.mult).then_inc(s("av", k), 1)
         ve.tensor_scalar(h[:, 1:4 * NC:4], bank(k, 0), -CS, 0.0, AluOpType.mult, AluOpType.max).then_inc(s("av", k), 1)
+        sc.wait_ge(s("zb", k), 1)
         sc.activation(h[:, 2:4 * NC:4], bank(k, 1), ActivationFunctionType.Relu, scale=CS).then_inc(s("as", k), 1)
         sc.activation(h[:, 3:4 * NC:4], bank(k, 1), ActivationFunctionType.Relu, scale=-CS).then_inc(s("as", k), 1)
-        ve.wait_ge(s("av", k), 2 * (m + 1))
-        ve.wait_ge(s("as", k), 2 * (m + 1))
-        if m:
-            ve.wait_ge(s("y", k), m)
-        ve.quantize_mx(T["hq%d" % (k % SETS)][:], T["hs%d" % (k % SETS)][:], h[:]).then_inc(s("hq", k), 1)
+
+    def quantise(k):
+        ve.wait_ge(s("av", k), 2)
+        ve.wait_ge(s("as", k), 2)
+        ve.quantize_mx(T["hq%d" % k][:], T["hs%d" % k][:], T["h%d" % k][:]).then_inc(s("hq", k), 1)
 
     def second_layer(k):
         a = slots[k] * WC + W1C
         if order[k][0] < 4:
             arrived(k, "b")
-        te.wait_ge(s("hq", k), k // SETS + 1)
+        te.wait_ge(s("hq", k), 1)
         te.matmul_mx(T.yacc[:, 0:NC], T.wq[:, a:a + 128], T.ws[:, a:a + 128],
-                     T["hq%d" % (k % SETS)][:], T["hs%d" % (k % SETS)][:], k == 0, k == N - 1).then_inc(s("y", k), 1)
+                     T["hq%d" % k][:], T["hs%d" % k][:], k == 0, k == N - 1).then_inc(sem.y, 1)
 
     for k in range(N):
         first_layer(k)
-        if k >= AHEAD:
-            second_layer(k - AHEAD)
-        tile(k)
-    for k in range(N - AHEAD, N):
+        if k == 1:
+            second_layer(0)
+        if k > LAG:
+            second_layer(k - LAG)
+    for k in range(N - LAG, N):
         second_layer(k)
-    for b in range(SETS):
-        ve.wait_ge(sem["y%d" % b], len(range(b, N, SETS)))
+    tile(0)
+    quantise(0)
+    tile(1)
+    for k in range(2, N):
+        tile(k)
+        quantise(k - 1)
+    quantise(N - 1)
+    ve.wait_ge(sem.y, N)
     ve.tensor_copy(T.ysb[:], T.yacc[:, 0:NC]).then_inc(sem.out, 1)
     g.sync.wait_ge(sem.out, 1)
     g.sync.dma_start(T.y[:], T.ysb[:]).then_inc(sem.done, 16)

import numpy as np
from concourse.bass import DstId, RemoteDMATransfer
from concourse.mybir import dt, AluOpType, ActivationFunctionType

N = 8
WORLD = 256
WC = 384
W1C = 256
NC = 256
CS = float(np.float32(0.043))
SETS = 3
LAG = 3

SCRATCH = {
    "wbf": ("sbuf", [128, 4 * WC], "bfloat16"),
    "xbf": ("sbuf", [128, 4 * NC], "bfloat16"),
    "xq": ("sbuf", [128, NC], "float8_e4m3fn_x4"),
    "xs": ("sbuf", [128, NC], "uint8"),
    "wq": ("sbuf", [128, N * WC], "float8_e4m3fn_x4"),
    "ws": ("sbuf", [128, N * WC], "uint8"),
    "ysb": ("sbuf", [128, NC], "float32"),
    "z": ("psum", [128, 512 * 2 * SETS], "float32"),
    "yacc": ("psum", [128, 512], "float32"),
}
for _b in range(N):
    SCRATCH["h%d" % _b] = ("sbuf", [128, 4 * NC], "bfloat16")
    SCRATCH["hq%d" % _b] = ("sbuf", [128, NC], "float8_e4m3fn_x4")
    SCRATCH["hs%d" % _b] = ("sbuf", [128, NC], "uint8")
SEMAPHORES = (["w1a", "w1b", "w2", "x", "wq0", "wq1", "wqb", "xq", "y", "out", "done", "loc"]
              + ["%s%d" % (n, b) for n in ("za", "zb", "av", "as", "hq") for b in range(N)]
              + ["%s%d" % (n, i) for n in ("a", "b", "c") for i in range(N)])


def _bits(mask):
    return [e for e in range(mask.bit_length()) if (mask >> e) & 1]


def _plan(cores, topo):
    cores = list(cores)
    own, fwd, relay = {}, {c: [] for c in cores}, {}
    cls = {c: [] for c in cores}

    def chipkey(c):
        return (topo.host(c), topo.chip(c))

    def groups(cs):
        out = {}
        for c in cs:
            out.setdefault(chipkey(c), []).append(c)
        return [out[k] for k in sorted(out)]

    def common(src, dsts):
        m = topo.mask(src, dsts[0])
        for d in dsts[1:]:
            m &= topo.mask(src, d)
        return _bits(m)

    for i, P in enumerate(cores):
        lo, hi = i * WC, (i + 1) * WC
        sa, sb, sc = "a%d" % i, "b%d" % i, "c%d" % i
        mid = lo + W1C // 2
        peers = [q for q in cores if q != P and chipkey(q) == chipkey(P)]
        plane = [q for q in cores if topo.same_plane(P, q)]
        cross = [q for q in cores if q != P and q not in peers and q not in plane]
        off = common(P, plane)
        on = [e for e in common(P, peers) if e not in off]
        cls[P].append((0, i))
        direct = [(peers, on)]
        for d in peers:
            cls[d].append((1, i))

        def split(grp):
            head = [d for d in grp if topo.die(d) == topo.die(P)][0]
            return head, [d for d in grp if d != head]

        for grp in groups(plane):
            head, rest = split(grp)
            direct.append(([head], off))
            cls[head].append((2, i))
            for a, b, sn, need, when in ((lo, lo + W1C, sa, (sa, sc), 2), (lo + W1C, hi, sb, (sb,), 5)):
                out = [(rest, common(head, rest), a, b, sn)]
                fwd[head].append((when, [(need, "p", out), ((), "c", out)]))
            for d in rest:
                cls[d].append((3, i))
        feed = []
        for grp in groups(cross):
            near = topo.host(grp[0]) == topo.host(P)
            head, rest = split(grp)
            if near:
                rel = [k for k in range(WORLD) if chipkey(k) == chipkey(P) and k not in cores]
            else:
                rel = [k for k in range(WORLD) if topo.mates(k, head) and k not in cores and topo.may_write(P, k)]
            rel = [k for k in rel if topo.die(k) == topo.die(P) and topo.may_write(k, head)][:2]
            pool = on if near else off
            ne, nc = len(pool) // len(rel), WC // len(rel)
            for t, k in enumerate(rel):
                a, b = lo + t * nc, lo + (t + 1) * nc
                feed.append((k, pool[t * ne:(t + 1) * ne], a, b))
                e = common(k, [head])
                relay[k] = [((sa,), "p", [([head], e, a, b, sa)]), ((sb,), "c", [([head], e, a, b, sb)])]
            e = common(head, rest)
            fwd[head].append((4 if near else 6,
                              [((sa,), "p", [(rest, e, lo, hi, sa)]), ((sb,), "c", [(rest, e, lo, hi, sb)])]))
            cls[head].append((4 if near else 5, i))
            for d in rest:
                cls[d].append((6 if near else 7, i))

        def straight(need, kind, a, b, sn):
            return (need, kind, [(dsts, engs, a, b, sn) for dsts, engs in direct])

        own[P] = [straight(("wq0",), "c", lo, mid, sa),
                  straight(("wq1",), "p", lo, lo + W1C, sa),
                  straight((), "c", mid, lo + W1C, sc),
                  (("wqb",), "p", [([k], e, a, b, sa) for k, e, a, b in feed]),
                  ((), "c", [([k], e, a, b, sb) for k, e, a, b in feed]),
                  straight((), "p", lo + W1C, hi, sb),
                  straight((), "c", lo + W1C, hi, sb)]

    steps = dict(relay)
    expect = {}
    for P in cores:
        steps[P] = own[P] + [st for _, sts in sorted(fwd[P], key=lambda f: f[0]) for st in sts]
        expect[(P, "wq0")] = expect[(P, "wq1")] = expect[(P, "wqb")] = 1
    for c in steps:
        for _, kind, trs in steps[c]:
            for dsts, engs, _, _, sn in trs:
                expect[(c, "loc")] = expect.get((c, "loc"), 0) + len(engs)
                for d in dsts:
                    expect[(d, sn)] = expect.get((d, sn), 0) + len(engs)
    order = {c: sorted(cls[c]) for c in cores}
    return steps, expect, order


def _remote(g, core, T, topo, steps, expect):
    for waits, kind, trs in steps:
        for wait in waits:
            g.wait_ge(T.sem[wait], expect[(core, wait)])
        calls = []
        for dsts, engs, a, b, sn in trs:
            def view():
                return T.ws[:, a:b] if kind == "p" else T.wq[:, a:b].bitcast(dt.uint8)
            ids = []
            for d in dsts:
                rid, pid = topo.addr(d, core)
                ids.append(DstId(rid=rid, pnc=pid))
            calls.append(RemoteDMATransfer(dst_ids=ids, dma_engine_mask=sum(1 << e for e in engs),
                                           remote_sem=T.sem[sn], srcs=[view()], dsts=[view() for _ in dsts]))
        g.remote_dma_fused(calls, local_sem=T.sem.loc)
    g.wait_ge(T.sem.loc, expect[(core, "loc")])


def _compute(g, core, T, order, expect):
    sem, te, ve, sc = T.sem, g.tensor, g.vector, g.scalar
    slots = [sl for _, sl in order]
    o = slots[0] * WC
    H = W1C // 2
    g.sync.dma_start(T.wbf[:, 0:4 * H], T.w1[:, 0:4 * H]).then_inc(sem.w1a, 16)
    g.sync.dma_start(T.wbf[:, 4 * H:4 * W1C], T.w1[:, 4 * H:4 * W1C]).then_inc(sem.w1b, 16)
    g.sync.dma_start(T.wbf[:, 4 * W1C:4 * WC], T.w2[:]).then_inc(sem.w2, 16)
    g.sync.dma_start(T.xbf[:], T.x[:]).then_inc(sem.x, 16)
    ve.wait_ge(sem.w1a, 16)
    ve.quantize_mx(T.wq[:, o:o + H], T.ws[:, o:o + H], T.wbf[:, 0:4 * H]).then_inc(sem.wq0, 1)
    ve.wait_ge(sem.w1b, 16)
    ve.quantize_mx(T.wq[:, o + H:o + W1C], T.ws[:, o + H:o + W1C], T.wbf[:, 4 * H:4 * W1C]).then_inc(sem.wq1, 1)
    ve.wait_ge(sem.w2, 16)
    ve.quantize_mx(T.wq[:, o + W1C:o + WC], T.ws[:, o + W1C:o + WC], T.wbf[:, 4 * W1C:4 * WC]).then_inc(sem.wqb, 1)
    ve.wait_ge(sem.x, 16)
    ve.quantize_mx(T.xq[:], T.xs[:], T.xbf[:]).then_inc(sem.xq, 1)

    def s(name, k):
        return sem["%s%d" % (name, k)]

    def bank(k, i):
        c = 512 * (2 * (k % SETS) + i)
        return T.z[:, c:c + NC]

    def arrived(k, part):
        name = {"a": "wq0", "c": "wq1", "b": "wqb"}[part] if k == 0 else "%s%d" % (part, slots[k])
        te.wait_ge(sem[name], expect[(core, name)])

    def first_layer(k):
        w = slots[k] * WC
        arrived(k, "a")
        if order[k][0] >= 4:
            arrived(k, "b")
        if k == 0:
            te.wait_ge(sem.xq, 1)
        for i, (free, made) in enumerate((("av", "za"), ("as", "zb"))):
            if i == 1 and order[k][0] <= 2:
                arrived(k, "c")
            if k >= SETS:
                te.wait_ge(s(free, k - SETS), 2)
            a = w + 128 * i
            te.matmul_mx(bank(k, i), T.wq[:, a:a + 128], T.ws[:, a:a + 128], T.xq[:], T.xs[:], True, True
                         ).then_inc(s(made, k), 1)

    def tile(k):
        h = T["h%d" % k]
        ve.wait_ge(s("za", k), 1)
        ve.tensor_scalar(h[:, 0:4 * NC:4], bank(k, 0), 0.0, CS, AluOpType.max, AluOpType.mult).then_inc(s("av", k), 1)
        ve.tensor_scalar(h[:, 1:4 * NC:4], bank(k, 0), -CS, 0.0, AluOpType.mult, AluOpType.max).then_inc(s("av", k), 1)
        sc.wait_ge(s("zb", k), 1)
        sc.activation(h[:, 2:4 * NC:4], bank(k, 1), ActivationFunctionType.Relu, scale=CS).then_inc(s("as", k), 1)
        sc.activation(h[:, 3:4 * NC:4], bank(k, 1), ActivationFunctionType.Relu, scale=-CS).then_inc(s("as", k), 1)

    def quantise(k):
        ve.wait_ge(s("av", k), 2)
        ve.wait_ge(s("as", k), 2)
        ve.quantize_mx(T["hq%d" % k][:], T["hs%d" % k][:], T["h%d" % k][:]).then_inc(s("hq", k), 1)

    def second_layer(k):
        a = slots[k] * WC + W1C
        if order[k][0] < 4:
            arrived(k, "b")
        te.wait_ge(s("hq", k), 1)
        te.matmul_mx(T.yacc[:, 0:NC], T.wq[:, a:a + 128], T.ws[:, a:a + 128],
                     T["hq%d" % k][:], T["hs%d" % k][:], k == 0, k == N - 1).then_inc(sem.y, 1)

    for k in range(N):
        first_layer(k)
        if k == 1:
            second_layer(0)
        if k > LAG:
            second_layer(k - LAG)
    for k in range(N - LAG, N):
        second_layer(k)
    tile(0)
    quantise(0)
    tile(1)
    for k in range(2, N):
        tile(k)
        quantise(k - 1)
    quantise(N - 1)
    ve.wait_ge(sem.y, N)
    ve.tensor_copy(T.ysb[:], T.yacc[:, 0:NC]).then_inc(sem.out, 1)
    g.sync.wait_ge(sem.out, 1)
    g.sync.dma_start(T.y[:], T.ysb[:]).then_inc(sem.done, 16)
    g.sync.wait_ge(sem.done, 16)


def rank_program(g, core, T, topo):
    steps, expect, order = _plan(T.cores, topo)
    if core not in steps:
        return
    if T.rank_of(core) is not None:
        _compute(g, core, T, order[core], expect)
    _remote(g, core, T, topo, steps[core], expect)
